import numpy as np
import ml_dtypes


def mxq(x, axis, fmt="e4m3"):
    dtype, down = {"e4m3": (ml_dtypes.float8_e4m3fn, 7), "e5m2": (ml_dtypes.float8_e5m2, 14)}[fmt]
    v = np.moveaxis(np.asarray(x, np.float32).astype(ml_dtypes.bfloat16).astype(np.float64), axis, -1)
    blocks = v.reshape(v.shape[:-1] + (-1, 32))
    amax = np.abs(blocks).max(-1, keepdims=True)
    byte = np.maximum(np.where(amax > 0, np.frexp(amax)[1] - 1 + 127, 0) - down, 1)
    scale = np.exp2(byte - 127.0)
    codes = (blocks / scale).astype(np.float32).astype(dtype).astype(np.float64)
    return np.moveaxis((codes * scale).reshape(v.shape), -1, axis)


WIDE = False


def mx_kscale(k):
    if not WIDE:
        return np.ones(k)
    levels = np.array([10, -10, 5, -5, 0])
    if k % 512:
        return np.exp2(np.random.permutation(np.resize(levels, k // 32))).repeat(32)
    a = np.empty((k // 512, 16))
    for p in range(k // 512):
        a[p, :8] = np.random.permutation(np.resize(levels, 8))
        for g in range(8):
            far = levels[np.abs(levels - a[p, g]) >= 10]
            a[p, g + 8] = far[np.random.randint(len(far))]
    return np.exp2(a.ravel()).repeat(32)


def f64(x):
    return np.asarray(x).astype(np.float64)


def striped(idx):
    return np.tile(idx.reshape(-1, 16).T, (8, 1)).astype(np.uint16)


def unstriped(offs):
    return offs[:16].T.reshape(-1).astype(np.int64)


def silu(v):
    return v / (1.0 + np.exp(-np.maximum(v, -700.0)))


K, T, E, C, H, N = 1024, 2048, 2, 256, 512, 128


def by_expert(wq, xq):
    return np.concatenate([wq[e].T @ xq[:, e * C:(e + 1) * C] for e in range(E)], axis=1)


def setup_inputs():
    n = np.random.standard_normal
    s = mx_kscale(K)[:, None]
    u = mx_kscale(H)
    return {
        "xT": (n((K, T)) * s).astype(np.float32),
        "w1": (n((E, K, H)) / np.sqrt(K) / s[None]).astype(np.float32),
        "w3": (n((E, K, H)) / np.sqrt(K) / s[None] * u[None, None, :]).astype(np.float32),
        "w2": (n((E, H, N)) / np.sqrt(H) / u[None, :, None]).astype(np.float32),
        "gate": np.tile(np.random.uniform(0.2, 1.0, E * C), (N, 1)).astype(np.float32),
        "offs": striped(np.random.permutation(T)[:E * C]),
    }


def reference(xT, w1, w3, w2, gate, offs):
    idx = unstriped(offs)
    xq = mxq(f64(xT)[:, idx], 0, "e4m3")
    h = silu(by_expert(mxq(f64(w1), 1, "e4m3"), xq))
    h = h * by_expert(mxq(f64(w3), 1, "e4m3"), xq)
    y = by_expert(mxq(f64(w2), 1, "e4m3"), mxq(h, 0, "e4m3"))
    out = np.zeros((N, T))
    out[:, idx] = f64(gate) * y
    return out

@@ -1,0 +1,238 @@
+from contextlib import ExitStack
+
+import concourse.mybir as mybir
+
+K, T, E, C, H, N = 1024, 2048, 2, 256, 512, 128
+FLOPS = 2 * E * C * (2 * K * H + H * N)
+
+F32 = mybir.dt.float32
+BF16 = mybir.dt.bfloat16
+U32 = mybir.dt.uint32
+U16 = mybir.dt.uint16
+U8 = mybir.dt.uint8
+FP8X4 = mybir.dt.float8_e4m3fn_x4
+MULT = mybir.AluOpType.mult
+SILU = mybir.ActivationFunctionType.Silu
+
+P = 128
+PACK = 4
+K_PASS = P * PACK
+PASSES = K // K_PASS
+SLOTS = E * C
+HALF = 128
+HALVES = C // HALF
+
+W1, W3 = 0, 1
+CHUNKS = (
+    (0, W1, 0), (0, W3, 0), (0, W1, 1), (0, W3, 1),
+    (1, W1, 0), (1, W3, 0), (1, W1, 1), (1, W3, 1),
+)
+CHUNK_VECTOR_SHARE = (64, 64, 64, 64, 32, 32, 64, 88)
+TOKEN_VECTOR_SHARE = 64
+
+
+def shared_copy(nc, dst, src, vector_share):
+    nc.vector.tensor_copy(out=dst[:, 0:vector_share, :, :], in_=src[:, 0:vector_share, :, :])
+    nc.scalar.copy(out=dst[:, vector_share:, :, :], in_=src[:, vector_share:, :, :])
+
+
+def tile_routed_moe_kernel(tc, xT, w1, w3, w2, gate, offs, out):
+    nc = tc.nc
+    with ExitStack() as ctx:
+        keep = ctx.enter_context(tc.tile_pool(name="keep", bufs=1))
+        work = ctx.enter_context(tc.tile_pool(name="work", bufs=2))
+        wgp = ctx.enter_context(tc.tile_pool(name="wgp", bufs=3))
+        hp = ctx.enter_context(tc.tile_pool(name="hp", bufs=4))
+        psum = ctx.enter_context(tc.psum_pool(name="psum", bufs=2))
+
+        x_plane = {}
+        w_raw = {}
+        w2_raw = {}
+        planes = xT.rearrange("(g p t) n -> g p t n", p=P, t=PACK)
+
+        def load_tokens(g):
+            for t in range(PACK):
+                x_plane[g, t] = keep.tile([P, T], F32, name="x_plane_%d_%d" % (g, t))
+                nc.sync.dma_start(out=x_plane[g, t][:], in_=planes[g, :, t, :])
+
+        def load_chunk(index):
+            e, mat, g = CHUNKS[index]
+            w_raw[index] = keep.tile([P, PACK, H], F32, name="w_raw_%d" % index)
+            rows = (w1, w3)[mat][e, g * K_PASS:(g + 1) * K_PASS, :]
+            nc.sync.dma_start(out=w_raw[index][:], in_=rows.rearrange("(p j) c -> p j c", j=PACK))
+
+        def load_w2():
+            for e in range(E):
+                w2_raw[e] = keep.tile([P, PACK, N], F32, name="w2_raw_%d" % e)
+                nc.sync.dma_start(out=w2_raw[e][:], in_=w2[e].rearrange("(p j) n -> p j n", j=PACK))
+
+        offs_sb = keep.tile([P, SLOTS // 16], U16, name="offs_sb")
+        nc.sync.dma_start(offs_sb[:], offs)
+        load_tokens(0)
+        load_chunk(0)
+        load_chunk(1)
+        load_tokens(1)
+        load_chunk(2)
+        load_chunk(3)
+        load_w2()
+        for index in range(4, 8):
+            load_chunk(index)
+        gate_sb = keep.tile([P, SLOTS], F32, name="gate_sb")
+        nc.sync.dma_start(out=gate_sb[:], in_=gate)
+
+        warm_in = keep.tile([P, 1], F32, name="warm_in")
+        warm_out = keep.tile([P, 1], F32, name="warm_out")
+        nc.vector.memset(warm_in[:], 0.0)
+        nc.scalar.activation(out=warm_out[:], in_=warm_in[:], func=SILU)
+        win = keep.tile([P, T], F32, name="win")
+        nc.vector.memset(win[:], 0.0)
+
+        x_codes = {}
+        x_scales = {}
+        w2_codes = {}
+        w2_scales = {}
+        w_codes = {}
+        w_scales = {}
+        sil = {}
+        y_bank = {}
+
+        def tokens(g):
+            g4 = work.tile([P, PACK, SLOTS], F32, name="g4")
+            for t in range(PACK):
+                nc.vector.tensor_copy(g4[:, t, :], x_plane[g, t][:].indirect(offs_sb[:]))
+            xg = work.tile([P, SLOTS, PACK], BF16, name="xg", align_bytes=64)
+            shared_copy(
+                nc,
+                xg[:].rearrange("p (c i) t -> p c t i", i=4),
+                g4[:].rearrange("p t (c i) -> p c t i", i=4),
+                TOKEN_VECTOR_SHARE,
+            )
+            x_codes[g] = keep.tile([P, SLOTS], U32, name="x_codes_%d" % g, align_bytes=64)
+            x_scales[g] = keep.tile([P, SLOTS], U8, name="x_scales_%d" % g, align_bytes=64)
+            nc.vector.quantize_mx(
+                out=x_codes[g][:].bitcast(FP8X4),
+                scales=x_scales[g][:],
+                in_=xg[:].rearrange("p c t -> p (c t)"),
+            )
+
+        def quantise_w2(e):
+            w2g = work.tile([P, N, PACK], BF16, name="w2g", align_bytes=64)
+            nc.vector.tensor_copy(
+                out=w2g[:].rearrange("p (c i) j -> p c j i", i=4),
+                in_=w2_raw[e][:].rearrange("p j (c i) -> p c j i", i=4),
+            )
+            w2_codes[e] = keep.tile([P, N], U32, name="w2_codes_%d" % e, align_bytes=64)
+            w2_scales[e] = keep.tile([P, N], U8, name="w2_scales_%d" % e, align_bytes=64)
+            nc.vector.quantize_mx(
+                out=w2_codes[e][:].bitcast(FP8X4),
+                scales=w2_scales[e][:],
+                in_=w2g[:].rearrange("p c j -> p (c j)"),
+            )
+
+        def quantise_chunk(index):
+            wg = wgp.tile([P, H, PACK], BF16, name="wg", align_bytes=64)
+            shared_copy(
+                nc,
+                wg[:].rearrange("p (s m) j -> p m j s", s=PACK),
+                w_raw[index][:].rearrange("p j (m s) -> p m j s", s=PACK),
+                CHUNK_VECTOR_SHARE[index],
+            )
+            key = CHUNKS[index]
+            w_codes[key] = keep.tile([P, H], U32, name="w_codes_%d" % index, align_bytes=64)
+            w_scales[key] = keep.tile([P, H], U8, name="w_scales_%d" % index, align_bytes=64)
+            nc.vector.quantize_mx(
+                out=w_codes[key][:].bitcast(FP8X4),
+                scales=w_scales[key][:],
+                in_=wg[:].rearrange("p c j -> p (c j)"),
+            )
+
+        def first_layer(e, mat, hf, name):
+            bank = psum.tile([P, PACK, HALF], F32, name=name)
+            cols = slice(e * C + hf * HALF, e * C + (hf + 1) * HALF)
+            for s in range(PACK):
+                for g in range(PASSES):
+                    nc.tensor.matmul_mx(
+                        out=bank[:, s, :],
+                        lhsT=w_codes[e, mat, g][:, s * P:(s + 1) * P].bitcast(FP8X4),
+                        lhsT_scale=w_scales[e, mat, g][:, s * P:(s + 1) * P],
+                        rhs=x_codes[g][:, cols].bitcast(FP8X4),
+                        rhs_scale=x_scales[g][:, cols],
+                        start=(g == 0),
+                        stop=(g == PASSES - 1),
+                    )
+            return bank
+
+        def silu(e, hf, a_bank, dst):
+            nc.scalar.activation(out=dst, in_=a_bank[:].rearrange("p s n -> p (s n)"), func=SILU)
+            sil[e, hf] = dst.rearrange("p (s n) -> p n s", s=PACK)
+
+        def second_layer(e, hf):
+            b_bank = first_layer(e, W3, hf, "b_bank")
+            hg = hp.tile([P, HALF, PACK], BF16, name="hg", align_bytes=64)
+            nc.vector.tensor_tensor(
+                out=hg[:],
+                in0=sil[e, hf],
+                in1=b_bank[:].rearrange("p s n -> p n s"),
+                op=MULT,
+            )
+            h_codes = hp.tile([P, HALF], U32, name="h_codes", align_bytes=64)
+            h_scales = hp.tile([P, HALF], U8, name="h_scales", align_bytes=64)
+            nc.vector.quantize_mx(
+                out=h_codes[:].bitcast(FP8X4),
+                scales=h_scales[:],
+                in_=hg[:].rearrange("p n s -> p (n s)"),
+            )
+            nc.tensor.matmul_mx(
+                out=y_bank[e][:, hf * HALF:(hf + 1) * HALF],
+                lhsT=w2_codes[e][:].bitcast(FP8X4),
+                lhsT_scale=w2_scales[e][:],
+                rhs=h_codes[:].bitcast(FP8X4),
+                rhs_scale=h_scales[:],
+                start=True,
+                stop=True,
+            )
+
+        def scatter(e, y_sb):
+            nc.vector.tensor_tensor(
+                win[:].indirect(offs_sb[:, e * (C // 16):(e + 1) * (C // 16)]),
+                y_sb,
+                gate_sb[:, e * C:(e + 1) * C],
+                MULT,
+            )
+
+        tokens(0)
+        quantise_chunk(0)
+        quantise_chunk(1)
+        tokens(1)
+        quantise_chunk(2)
+        for hf in range(HALVES):
+            a_bank = first_layer(0, W1, hf, "a_bank")
+            sil_0 = hp.tile([P, PACK * HALF], F32, name="sil_0")
+            silu(0, hf, a_bank, sil_0[:])
+        quantise_chunk(3)
+        quantise_w2(0)
+        quantise_w2(1)
+        y_bank[0] = psum.tile([P, C], F32, name="y_bank")
+        second_layer(0, 0)
+        second_layer(0, 1)
+        quantise_chunk(4)
+        quantise_chunk(5)
+        quantise_chunk(6)
+        a_banks = {}
+        for hf in range(HALVES):
+            a_banks[hf] = first_layer(1, W1, hf, "a_bank")
+        quantise_chunk(7)
+        late = keep.tile([P, HALVES * PACK * HALF + C], F32, name="late", tag="w_raw_7")
+        y_sb_0 = late[:, HALVES * PACK * HALF:]
+        nc.scalar.copy(out=y_sb_0, in_=y_bank[0][:])
+        for hf in range(HALVES):
+            silu(1, hf, a_banks[hf], late[:, hf * PACK * HALF:(hf + 1) * PACK * HALF])
+        y_bank[1] = psum.tile([P, C], F32, name="y_bank")
+        second_layer(1, 0)
+        scatter(0, y_sb_0)
+        second_layer(1, 1)
+        y_sb_1 = keep.tile([P, C], F32, name="y_sb_1")
+        nc.scalar.copy(out=y_sb_1[:], in_=y_bank[1][:])
+        scatter(1, y_sb_1[:])
+
+        nc.sync.dma_start(out=out, in_=win[:])

@@ -27,7 +27,9 @@ CHUNKS = (
     (0, W1, 0), (0, W3, 0), (0, W1, 1), (0, W3, 1),
     (1, W1, 0), (1, W3, 0), (1, W1, 1), (1, W3, 1),
 )
-CHUNK_VECTOR_SHARE = (64, 64, 64, 64, 32, 32, 64, 88)
+CHUNK_VECTOR_SHARE = (64, 64, 64, 64, 32, 32, 64)
+LAST = 7
+LAST_VECTOR_SHARE = (32, 48)
 TOKEN_VECTOR_SHARE = 64
 
 
@@ -48,6 +50,7 @@ def tile_routed_moe_kernel(tc, xT, w1, w3, w2, gate, offs, out):
         x_plane = {}
         w_raw = {}
         w2_raw = {}
+        last_raw = {}
         planes = xT.rearrange("(g p t) n -> g p t n", p=P, t=PACK)
 
         def load_tokens(g):
@@ -60,6 +63,16 @@ def tile_routed_moe_kernel(tc, xT, w1, w3, w2, gate, offs, out):
             w_raw[index] = keep.tile([P, PACK, H], F32, name="w_raw_%d" % index)
             rows = (w1, w3)[mat][e, g * K_PASS:(g + 1) * K_PASS, :]
             nc.sync.dma_start(out=w_raw[index][:], in_=rows.rearrange("(p j) c -> p j c", j=PACK))
+
+        def load_last():
+            e, mat, g = CHUNKS[LAST]
+            rows = (w1, w3)[mat][e, g * K_PASS:(g + 1) * K_PASS, :]
+            for part in range(2):
+                last_raw[part] = keep.tile([P, PACK, H // 2], F32, name="last_raw_%d" % part)
+                nc.sync.dma_start(
+                    out=last_raw[part][:],
+                    in_=rows[:, part * (H // 2):(part + 1) * (H // 2)].rearrange("(p j) c -> p j c", j=PACK),
+                )
 
         def load_w2():
             for e in range(E):
@@ -75,8 +88,9 @@ def tile_routed_moe_kernel(tc, xT, w1, w3, w2, gate, offs, out):
         load_chunk(2)
         load_chunk(3)
         load_w2()
-        for index in range(4, 8):
+        for index in range(4, 7):
             load_chunk(index)
+        load_last()
         gate_sb = keep.tile([P, SLOTS], F32, name="gate_sb")
         nc.sync.dma_start(out=gate_sb[:], in_=gate)
 
@@ -140,6 +154,25 @@ def tile_routed_moe_kernel(tc, xT, w1, w3, w2, gate, offs, out):
             key = CHUNKS[index]
             w_codes[key] = keep.tile([P, H], U32, name="w_codes_%d" % index, align_bytes=64)
             w_scales[key] = keep.tile([P, H], U8, name="w_scales_%d" % index, align_bytes=64)
+            nc.vector.quantize_mx(
+                out=w_codes[key][:].bitcast(FP8X4),
+                scales=w_scales[key][:],
+                in_=wg[:].rearrange("p c j -> p (c j)"),
+            )
+
+        def quantise_last():
+            wg = wgp.tile([P, H, PACK], BF16, name="wg", align_bytes=64)
+            rows_of_m = P // 2
+            for part in range(2):
+                shared_copy(
+                    nc,
+                    wg[:].rearrange("p (s m) j -> p m j s", s=PACK)[:, part * rows_of_m:(part + 1) * rows_of_m, :, :],
+                    last_raw[part][:].rearrange("p j (m s) -> p m j s", s=PACK),
+                    LAST_VECTOR_SHARE[part],
+                )
+            key = CHUNKS[LAST]
+            w_codes[key] = keep.tile([P, H], U32, name="w_codes_%d" % LAST, align_bytes=64)
+            w_scales[key] = keep.tile([P, H], U8, name="w_scales_%d" % LAST, align_bytes=64)
             nc.vector.quantize_mx(
                 out=w_codes[key][:].bitcast(FP8X4),
                 scales=w_scales[key][:],
@@ -221,8 +254,8 @@ def tile_routed_moe_kernel(tc, xT, w1, w3, w2, gate, offs, out):
         a_banks = {}
         for hf in range(HALVES):
             a_banks[hf] = first_layer(1, W1, hf, "a_bank")
-        quantise_chunk(7)
-        late = keep.tile([P, HALVES * PACK * HALF + C], F32, name="late", tag="w_raw_7")
+        quantise_last()
+        late = keep.tile([P, HALVES * PACK * HALF + C], F32, name="late", tag="last_raw_1")
         y_sb_0 = late[:, HALVES * PACK * HALF:]
         nc.scalar.copy(out=y_sb_0, in_=y_bank[0][:])
         for hf in range(HALVES):

@@ -27,9 +27,7 @@ CHUNKS = (
     (0, W1, 0), (0, W3, 0), (0, W1, 1), (0, W3, 1),
     (1, W1, 0), (1, W3, 0), (1, W1, 1), (1, W3, 1),
 )
-CHUNK_VECTOR_SHARE = (64, 64, 64, 64, 32, 32, 64)
-LAST = 7
-LAST_VECTOR_SHARE = (32, 48)
+CHUNK_VECTOR_SHARE = ((64,), (64,), (64,), (64,), (32,), (32,), (32, 32), (32, 48))
 TOKEN_VECTOR_SHARE = 64
 
 
@@ -50,7 +48,6 @@ def tile_routed_moe_kernel(tc, xT, w1, w3, w2, gate, offs, out):
         x_plane = {}
         w_raw = {}
         w2_raw = {}
-        last_raw = {}
         planes = xT.rearrange("(g p t) n -> g p t n", p=P, t=PACK)
 
         def load_tokens(g):
@@ -60,18 +57,14 @@ def tile_routed_moe_kernel(tc, xT, w1, w3, w2, gate, offs, out):
 
         def load_chunk(index):
             e, mat, g = CHUNKS[index]
-            w_raw[index] = keep.tile([P, PACK, H], F32, name="w_raw_%d" % index)
             rows = (w1, w3)[mat][e, g * K_PASS:(g + 1) * K_PASS, :]
-            nc.sync.dma_start(out=w_raw[index][:], in_=rows.rearrange("(p j) c -> p j c", j=PACK))
-
-        def load_last():
-            e, mat, g = CHUNKS[LAST]
-            rows = (w1, w3)[mat][e, g * K_PASS:(g + 1) * K_PASS, :]
-            for part in range(2):
-                last_raw[part] = keep.tile([P, PACK, H // 2], F32, name="last_raw_%d" % part)
+            parts = len(CHUNK_VECTOR_SHARE[index])
+            width = H // parts
+            for part in range(parts):
+                w_raw[index, part] = keep.tile([P, PACK, width], F32, name="w_raw_%d_%d" % (index, part))
                 nc.sync.dma_start(
-                    out=last_raw[part][:],
-                    in_=rows[:, part * (H // 2):(part + 1) * (H // 2)].rearrange("(p j) c -> p j c", j=PACK),
+                    out=w_raw[index, part][:],
+                    in_=rows[:, part * width:(part + 1) * width].rearrange("(p j) c -> p j c", j=PACK),
                 )
 
         def load_w2():
@@ -88,9 +81,8 @@ def tile_routed_moe_kernel(tc, xT, w1, w3, w2, gate, offs, out):
         load_chunk(2)
         load_chunk(3)
         load_w2()
-        for index in range(4, 7):
+        for index in range(4, 8):
             load_chunk(index)
-        load_last()
         gate_sb = keep.tile([P, SLOTS], F32, name="gate_sb")
         nc.sync.dma_start(out=gate_sb[:], in_=gate)
 
@@ -145,34 +137,18 @@ def tile_routed_moe_kernel(tc, xT, w1, w3, w2, gate, offs, out):
 
         def quantise_chunk(index):
             wg = wgp.tile([P, H, PACK], BF16, name="wg", align_bytes=64)
-            shared_copy(
-                nc,
-                wg[:].rearrange("p (s m) j -> p m j s", s=PACK),
-                w_raw[index][:].rearrange("p j (m s) -> p m j s", s=PACK),
-                CHUNK_VECTOR_SHARE[index],
-            )
+            parts = len(CHUNK_VECTOR_SHARE[index])
+            m_rows = P // parts
+            for part in range(parts):
+                shared_copy(
+                    nc,
+                    wg[:].rearrange("p (s m) j -> p m j s", s=PACK)[:, part * m_rows:(part + 1) * m_rows, :, :],
+                    w_raw[index, part][:].rearrange("p j (m s) -> p m j s", s=PACK),
+                    CHUNK_VECTOR_SHARE[index][part],
+                )
             key = CHUNKS[index]
             w_codes[key] = keep.tile([P, H], U32, name="w_codes_%d" % index, align_bytes=64)
             w_scales[key] = keep.tile([P, H], U8, name="w_scales_%d" % index, align_bytes=64)
-            nc.vector.quantize_mx(
-                out=w_codes[key][:].bitcast(FP8X4),
-                scales=w_scales[key][:],
-                in_=wg[:].rearrange("p c j -> p (c j)"),
-            )
-
-        def quantise_last():
-            wg = wgp.tile([P, H, PACK], BF16, name="wg", align_bytes=64)
-            rows_of_m = P // 2
-            for part in range(2):
-                shared_copy(
-                    nc,
-                    wg[:].rearrange("p (s m) j -> p m j s", s=PACK)[:, part * rows_of_m:(part + 1) * rows_of_m, :, :],
-                    last_raw[part][:].rearrange("p j (m s) -> p m j s", s=PACK),
-                    LAST_VECTOR_SHARE[part],
-                )
-            key = CHUNKS[LAST]
-            w_codes[key] = keep.tile([P, H], U32, name="w_codes_%d" % LAST, align_bytes=64)
-            w_scales[key] = keep.tile([P, H], U8, name="w_scales_%d" % LAST, align_bytes=64)
             nc.vector.quantize_mx(
                 out=w_codes[key][:].bitcast(FP8X4),
                 scales=w_scales[key][:],
@@ -254,8 +230,8 @@ def tile_routed_moe_kernel(tc, xT, w1, w3, w2, gate, offs, out):
         a_banks = {}
         for hf in range(HALVES):
             a_banks[hf] = first_layer(1, W1, hf, "a_bank")
-        quantise_last()
-        late = keep.tile([P, HALVES * PACK * HALF + C], F32, name="late", tag="last_raw_1")
+        quantise_chunk(7)
+        late = keep.tile([P, HALVES * PACK * HALF + C], F32, name="late", tag="w_raw_7_1")
         y_sb_0 = late[:, HALVES * PACK * HALF:]
         nc.scalar.copy(out=y_sb_0, in_=y_bank[0][:])
         for hf in range(HALVES):

@@ -25,9 +25,9 @@ HALVES = C // HALF
 W1, W3 = 0, 1
 CHUNKS = (
     (0, W1, 0), (0, W3, 0), (0, W1, 1), (0, W3, 1),
-    (1, W1, 0), (1, W3, 0), (1, W1, 1), (1, W3, 1),
+    (1, W1, 0), (1, W1, 1), (1, W3, 0), (1, W3, 1),
 )
-CHUNK_VECTOR_SHARE = ((64,), (64,), (64,), (64,), (32,), (32,), (32, 32), (32, 48))
+CHUNK_VECTOR_SHARE = ((64,), (64,), (64,), (64,), (32,), (32,), (64,), (32, 48))
 TOKEN_VECTOR_SHARE = 64
 
 
@@ -226,10 +226,10 @@ def tile_routed_moe_kernel(tc, xT, w1, w3, w2, gate, offs, out):
         second_layer(0, 1)
         quantise_chunk(4)
         quantise_chunk(5)
-        quantise_chunk(6)
         a_banks = {}
         for hf in range(HALVES):
             a_banks[hf] = first_layer(1, W1, hf, "a_bank")
+        quantise_chunk(6)
         quantise_chunk(7)
         late = keep.tile([P, HALVES * PACK * HALF + C], F32, name="late", tag="w_raw_7_1")
         y_sb_0 = late[:, HALVES * PACK * HALF:]

@@ -27,7 +27,8 @@ CHUNKS = (
     (0, W1, 0), (0, W3, 0), (0, W1, 1), (0, W3, 1),
     (1, W1, 0), (1, W1, 1), (1, W3, 0), (1, W3, 1),
 )
-CHUNK_VECTOR_SHARE = ((64,), (64,), (64,), (64,), (32,), (32,), (64,), (32, 48))
+CHUNK_VECTOR_SHARE = ((64,), (64,), (64,), (64,), (32,), (32,), (64,), (56, 24))
+CHUNK_PIECE_ROWS = ((128,), (128,), (128,), (128,), (128,), (128,), (128,), (96, 32))
 TOKEN_VECTOR_SHARE = 64
 
 
@@ -58,14 +59,15 @@ def tile_routed_moe_kernel(tc, xT, w1, w3, w2, gate, offs, out):
         def load_chunk(index):
             e, mat, g = CHUNKS[index]
             rows = (w1, w3)[mat][e, g * K_PASS:(g + 1) * K_PASS, :]
-            parts = len(CHUNK_VECTOR_SHARE[index])
-            width = H // parts
-            for part in range(parts):
+            first = 0
+            for part, m_rows in enumerate(CHUNK_PIECE_ROWS[index]):
+                width = PACK * m_rows
                 w_raw[index, part] = keep.tile([P, PACK, width], F32, name="w_raw_%d_%d" % (index, part))
                 nc.sync.dma_start(
                     out=w_raw[index, part][:],
-                    in_=rows[:, part * width:(part + 1) * width].rearrange("(p j) c -> p j c", j=PACK),
+                    in_=rows[:, first:first + width].rearrange("(p j) c -> p j c", j=PACK),
                 )
+                first += width
 
         def load_w2():
             for e in range(E):
@@ -137,15 +139,15 @@ def tile_routed_moe_kernel(tc, xT, w1, w3, w2, gate, offs, out):
 
         def quantise_chunk(index):
             wg = wgp.tile([P, H, PACK], BF16, name="wg", align_bytes=64)
-            parts = len(CHUNK_VECTOR_SHARE[index])
-            m_rows = P // parts
-            for part in range(parts):
+            first = 0
+            for part, m_rows in enumerate(CHUNK_PIECE_ROWS[index]):
                 shared_copy(
                     nc,
-                    wg[:].rearrange("p (s m) j -> p m j s", s=PACK)[:, part * m_rows:(part + 1) * m_rows, :, :],
+                    wg[:].rearrange("p (s m) j -> p m j s", s=PACK)[:, first:first + m_rows, :, :],
                     w_raw[index, part][:].rearrange("p j (m s) -> p m j s", s=PACK),
                     CHUNK_VECTOR_SHARE[index][part],
                 )
+                first += m_rows
             key = CHUNKS[index]
             w_codes[key] = keep.tile([P, H], U32, name="w_codes_%d" % index, align_bytes=64)
             w_scales[key] = keep.tile([P, H], U8, name="w_scales_%d" % index, align_bytes=64)

@@ -193,8 +193,9 @@ def tile_routed_moe_kernel(tc, xT, w1, w3, w2, gate, offs, out):
                 scales=h_scales[:],
                 in_=hg[:].rearrange("p n s -> p (n s)"),
             )
+            y_bank[e, hf] = psum.tile([P, HALF], F32, name="y_bank")
             nc.tensor.matmul_mx(
-                out=y_bank[e][:, hf * HALF:(hf + 1) * HALF],
+                out=y_bank[e, hf][:],
                 lhsT=w2_codes[e][:].bitcast(FP8X4),
                 lhsT_scale=w2_scales[e][:],
                 rhs=h_codes[:].bitcast(FP8X4),
@@ -223,7 +224,6 @@ def tile_routed_moe_kernel(tc, xT, w1, w3, w2, gate, offs, out):
         quantise_chunk(3)
         quantise_w2(0)
         quantise_w2(1)
-        y_bank[0] = psum.tile([P, C], F32, name="y_bank")
         second_layer(0, 0)
         second_layer(0, 1)
         quantise_chunk(4)
@@ -235,15 +235,16 @@ def tile_routed_moe_kernel(tc, xT, w1, w3, w2, gate, offs, out):
         quantise_chunk(7)
         late = keep.tile([P, HALVES * PACK * HALF + C], F32, name="late", tag="w_raw_7_1")
         y_sb_0 = late[:, HALVES * PACK * HALF:]
-        nc.scalar.copy(out=y_sb_0, in_=y_bank[0][:])
+        for hf in range(HALVES):
+            nc.scalar.copy(out=y_sb_0[:, hf * HALF:(hf + 1) * HALF], in_=y_bank[0, hf][:])
         for hf in range(HALVES):
             silu(1, hf, a_banks[hf], late[:, hf * PACK * HALF:(hf + 1) * PACK * HALF])
-        y_bank[1] = psum.tile([P, C], F32, name="y_bank")
+        y_sb_1 = keep.tile([P, C], F32, name="y_sb_1")
         second_layer(1, 0)
+        nc.scalar.copy(out=y_sb_1[:, 0:HALF], in_=y_bank[1, 0][:])
         scatter(0, y_sb_0)
         second_layer(1, 1)
-        y_sb_1 = keep.tile([P, C], F32, name="y_sb_1")
-        nc.scalar.copy(out=y_sb_1[:], in_=y_bank[1][:])
+        nc.scalar.copy(out=y_sb_1[:, HALF:C], in_=y_bank[1, 1][:])
         scatter(1, y_sb_1[:])
 
         nc.sync.dma_start(out=out, in_=win[:])

@@ -27,7 +27,7 @@ CHUNKS = (
     (0, W1, 0), (0, W3, 0), (0, W1, 1), (0, W3, 1),
     (1, W1, 0), (1, W1, 1), (1, W3, 0), (1, W3, 1),
 )
-CHUNK_VECTOR_SHARE = ((64,), (64,), (64,), (64,), (32,), (32,), (64,), (56, 24))
+CHUNK_VECTOR_SHARE = ((64,), (64,), (64,), (64,), (96,), (32,), (64,), (56, 24))
 CHUNK_PIECE_ROWS = ((128,), (128,), (128,), (128,), (128,), (128,), (128,), (96, 32))
 TOKEN_VECTOR_SHARE = 64
 
@@ -62,7 +62,7 @@ def tile_routed_moe_kernel(tc, xT, w1, w3, w2, gate, offs, out):
             first = 0
             for part, m_rows in enumerate(CHUNK_PIECE_ROWS[index]):
                 width = PACK * m_rows
-                w_raw[index, part] = keep.tile([P, PACK, width], F32, name="w_raw_%d_%d" % (index, part))
+                w_raw[index, part] = keep.tile([P, PACK, width], F32, name="w_raw_%d_%d" % (index, part), align_bytes=64)
                 nc.sync.dma_start(
                     out=w_raw[index, part][:],
                     in_=rows[:, first:first + width].rearrange("(p j) c -> p j c", j=PACK),
@@ -102,6 +102,10 @@ def tile_routed_moe_kernel(tc, xT, w1, w3, w2, gate, offs, out):
         w_codes = {}
         w_scales = {}
         sil = {}
+        w2g = {}
+        wg = {}
+        b_bank = {}
+        hg = {}
         y_bank = {}
 
         def tokens(g):
@@ -123,38 +127,42 @@ def tile_routed_moe_kernel(tc, xT, w1, w3, w2, gate, offs, out):
                 in_=xg[:].rearrange("p c t -> p (c t)"),
             )
 
-        def quantise_w2(e):
-            w2g = work.tile([P, N, PACK], BF16, name="w2g", align_bytes=64)
+        def interleave_w2(e):
+            w2g[e] = work.tile([P, N, PACK], BF16, name="w2g", align_bytes=64)
             nc.vector.tensor_copy(
-                out=w2g[:].rearrange("p (c i) j -> p c j i", i=4),
+                out=w2g[e][:].rearrange("p (c i) j -> p c j i", i=4),
                 in_=w2_raw[e][:].rearrange("p j (c i) -> p c j i", i=4),
             )
+
+        def quantise_w2(e):
             w2_codes[e] = keep.tile([P, N], U32, name="w2_codes_%d" % e, align_bytes=64)
             w2_scales[e] = keep.tile([P, N], U8, name="w2_scales_%d" % e, align_bytes=64)
             nc.vector.quantize_mx(
                 out=w2_codes[e][:].bitcast(FP8X4),
                 scales=w2_scales[e][:],
-                in_=w2g[:].rearrange("p c j -> p (c j)"),
+                in_=w2g[e][:].rearrange("p c j -> p (c j)"),
             )
 
-        def quantise_chunk(index):
-            wg = wgp.tile([P, H, PACK], BF16, name="wg", align_bytes=64)
+        def interleave_chunk(index):
+            wg[index] = wgp.tile([P, H, PACK], BF16, name="wg", align_bytes=64)
             first = 0
             for part, m_rows in enumerate(CHUNK_PIECE_ROWS[index]):
                 shared_copy(
                     nc,
-                    wg[:].rearrange("p (s m) j -> p m j s", s=PACK)[:, first:first + m_rows, :, :],
+                    wg[index][:].rearrange("p (s m) j -> p m j s", s=PACK)[:, first:first + m_rows, :, :],
                     w_raw[index, part][:].rearrange("p j (m s) -> p m j s", s=PACK),
                     CHUNK_VECTOR_SHARE[index][part],
                 )
                 first += m_rows
+
+        def quantise_chunk(index):
             key = CHUNKS[index]
             w_codes[key] = keep.tile([P, H], U32, name="w_codes_%d" % index, align_bytes=64)
             w_scales[key] = keep.tile([P, H], U8, name="w_scales_%d" % index, align_bytes=64)
             nc.vector.quantize_mx(
                 out=w_codes[key][:].bitcast(FP8X4),
                 scales=w_scales[key][:],
-                in_=wg[:].rearrange("p c j -> p (c j)"),
+                in_=wg[index][:].rearrange("p c j -> p (c j)"),
             )
 
         def first_layer(e, mat, hf, name):
@@ -177,21 +185,21 @@ def tile_routed_moe_kernel(tc, xT, w1, w3, w2, gate, offs, out):
             nc.scalar.activation(out=dst, in_=a_bank[:].rearrange("p s n -> p (s n)"), func=SILU)
             sil[e, hf] = dst.rearrange("p (s n) -> p n s", s=PACK)
 
-        def second_layer(e, hf):
-            b_bank = first_layer(e, W3, hf, "b_bank")
-            hg = hp.tile([P, HALF, PACK], BF16, name="hg", align_bytes=64)
+        def hidden(e, hf):
             nc.vector.tensor_tensor(
-                out=hg[:],
+                out=hg[e, hf],
                 in0=sil[e, hf],
-                in1=b_bank[:].rearrange("p s n -> p n s"),
+                in1=b_bank[e, hf][:].rearrange("p s n -> p n s"),
                 op=MULT,
             )
+
+        def second_layer(e, hf):
             h_codes = hp.tile([P, HALF], U32, name="h_codes", align_bytes=64)
             h_scales = hp.tile([P, HALF], U8, name="h_scales", align_bytes=64)
             nc.vector.quantize_mx(
                 out=h_codes[:].bitcast(FP8X4),
                 scales=h_scales[:],
-                in_=hg[:].rearrange("p n s -> p (n s)"),
+                in_=hg[e, hf].rearrange("p n s -> p (n s)"),
             )
             y_bank[e, hf] = psum.tile([P, HALF], F32, name="y_bank")
             nc.tensor.matmul_mx(
@@ -213,38 +221,57 @@ def tile_routed_moe_kernel(tc, xT, w1, w3, w2, gate, offs, out):
             )
 
         tokens(0)
-        quantise_chunk(0)
-        quantise_chunk(1)
+        for index in (0, 1):
+            interleave_chunk(index)
+            quantise_chunk(index)
         tokens(1)
+        interleave_chunk(2)
         quantise_chunk(2)
         for hf in range(HALVES):
             a_bank = first_layer(0, W1, hf, "a_bank")
             sil_0 = hp.tile([P, PACK * HALF], F32, name="sil_0")
             silu(0, hf, a_bank, sil_0[:])
+        interleave_chunk(3)
         quantise_chunk(3)
-        quantise_w2(0)
-        quantise_w2(1)
-        second_layer(0, 0)
-        second_layer(0, 1)
+        for e in range(E):
+            interleave_w2(e)
+        for e in range(E):
+            quantise_w2(e)
+        for hf in range(HALVES):
+            b_bank[0, hf] = first_layer(0, W3, hf, "b_bank")
+        interleave_chunk(4)
+        hg_0 = keep.tile([P, HALVES, HALF, PACK], BF16, name="hg_0", tag="w_raw_4_0", align_bytes=64)
+        for hf in range(HALVES):
+            hg[0, hf] = hg_0[:, hf, :, :]
+            hidden(0, hf)
+        for hf in range(HALVES):
+            second_layer(0, hf)
         quantise_chunk(4)
+        interleave_chunk(5)
         quantise_chunk(5)
         a_banks = {}
         for hf in range(HALVES):
             a_banks[hf] = first_layer(1, W1, hf, "a_bank")
-        quantise_chunk(6)
-        quantise_chunk(7)
-        late = keep.tile([P, HALVES * PACK * HALF + C], F32, name="late", tag="w_raw_7_1")
+        for index in (6, 7):
+            interleave_chunk(index)
+            quantise_chunk(index)
+        late = keep.tile([P, HALVES * PACK * HALF + C], F32, name="late", tag="w_raw_7_1", align_bytes=64)
         y_sb_0 = late[:, HALVES * PACK * HALF:]
         for hf in range(HALVES):
             nc.scalar.copy(out=y_sb_0[:, hf * HALF:(hf + 1) * HALF], in_=y_bank[0, hf][:])
         for hf in range(HALVES):
             silu(1, hf, a_banks[hf], late[:, hf * PACK * HALF:(hf + 1) * PACK * HALF])
         y_sb_1 = keep.tile([P, C], F32, name="y_sb_1")
-        second_layer(1, 0)
-        nc.scalar.copy(out=y_sb_1[:, 0:HALF], in_=y_bank[1, 0][:])
+        for hf in range(HALVES):
+            b_bank[1, hf] = first_layer(1, W3, hf, "b_bank")
         scatter(0, y_sb_0)
-        second_layer(1, 1)
-        nc.scalar.copy(out=y_sb_1[:, HALF:C], in_=y_bank[1, 1][:])
+        for hf in range(HALVES):
+            hg_1 = hp.tile([P, HALF, PACK], BF16, name="hg_1", align_bytes=64)
+            hg[1, hf] = hg_1[:]
+            hidden(1, hf)
+        for hf in range(HALVES):
+            second_layer(1, hf)
+            nc.scalar.copy(out=y_sb_1[:, hf * HALF:(hf + 1) * HALF], in_=y_bank[1, hf][:])
         scatter(1, y_sb_1[:])
 
         nc.sync.dma_start(out=out, in_=win[:])

@@ -182,8 +182,8 @@ def tile_routed_moe_kernel(tc, xT, w1, w3, w2, gate, offs, out):
             return bank
 
         def silu(e, hf, a_bank, dst):
-            nc.scalar.activation(out=dst, in_=a_bank[:].rearrange("p s n -> p (s n)"), func=SILU)
-            sil[e, hf] = dst.rearrange("p (s n) -> p n s", s=PACK)
+            sil[e, hf] = dst.rearrange("p (n s) -> p n s", s=PACK)
+            nc.scalar.activation(out=sil[e, hf], in_=a_bank[:].rearrange("p s n -> p n s"), func=SILU)
 
         def hidden(e, hf):
             nc.vector.tensor_tensor(

@@ -27,9 +27,9 @@ CHUNKS = (
     (0, W1, 0), (0, W3, 0), (0, W1, 1), (0, W3, 1),
     (1, W1, 0), (1, W1, 1), (1, W3, 0), (1, W3, 1),
 )
-CHUNK_VECTOR_SHARE = ((64,), (64,), (64,), (64,), (96,), (32,), (64,), (56, 24))
+CHUNK_VECTOR_SHARE = ((64,), (64,), (64,), (64,), (112,), (32,), (64,), (56, 16))
 CHUNK_PIECE_ROWS = ((128,), (128,), (128,), (128,), (128,), (128,), (128,), (96, 32))
-TOKEN_VECTOR_SHARE = 64
+TOKEN_VECTOR_SHARE = (64, 96)
 
 
 def shared_copy(nc, dst, src, vector_share):
@@ -117,7 +117,7 @@ def tile_routed_moe_kernel(tc, xT, w1, w3, w2, gate, offs, out):
                 nc,
                 xg[:].rearrange("p (c i) t -> p c t i", i=4),
                 g4[:].rearrange("p t (c i) -> p c t i", i=4),
-                TOKEN_VECTOR_SHARE,
+                TOKEN_VECTOR_SHARE[g],
             )
             x_codes[g] = keep.tile([P, SLOTS], U32, name="x_codes_%d" % g, align_bytes=64)
             x_scales[g] = keep.tile([P, SLOTS], U8, name="x_scales_%d" % g, align_bytes=64)

@@ -69,10 +69,9 @@ def tile_routed_moe_kernel(tc, xT, w1, w3, w2, gate, offs, out):
                 )
                 first += width
 
-        def load_w2():
-            for e in range(E):
-                w2_raw[e] = keep.tile([P, PACK, N], F32, name="w2_raw_%d" % e)
-                nc.sync.dma_start(out=w2_raw[e][:], in_=w2[e].rearrange("(p j) n -> p j n", j=PACK))
+        def load_w2(e):
+            w2_raw[e] = keep.tile([P, PACK, N], F32, name="w2_raw_%d" % e)
+            nc.sync.dma_start(out=w2_raw[e][:], in_=w2[e].rearrange("(p j) n -> p j n", j=PACK))
 
         offs_sb = keep.tile([P, SLOTS // 16], U16, name="offs_sb")
         nc.sync.dma_start(offs_sb[:], offs)
@@ -82,9 +81,10 @@ def tile_routed_moe_kernel(tc, xT, w1, w3, w2, gate, offs, out):
         load_tokens(1)
         load_chunk(2)
         load_chunk(3)
-        load_w2()
+        load_w2(0)
         for index in range(4, 8):
             load_chunk(index)
+        load_w2(1)
         gate_sb = keep.tile([P, SLOTS], F32, name="gate_sb")
         nc.sync.dma_start(out=gate_sb[:], in_=gate)
 
@@ -127,9 +127,9 @@ def tile_routed_moe_kernel(tc, xT, w1, w3, w2, gate, offs, out):
                 in_=xg[:].rearrange("p c t -> p (c t)"),
             )
 
-        def interleave_w2(e):
+        def interleave_w2(e, copy):
             w2g[e] = work.tile([P, N, PACK], BF16, name="w2g", align_bytes=64)
-            nc.vector.tensor_copy(
+            copy(
                 out=w2g[e][:].rearrange("p (c i) j -> p c j i", i=4),
                 in_=w2_raw[e][:].rearrange("p j (c i) -> p c j i", i=4),
             )
@@ -233,10 +233,8 @@ def tile_routed_moe_kernel(tc, xT, w1, w3, w2, gate, offs, out):
             silu(0, hf, a_bank, sil_0[:])
         interleave_chunk(3)
         quantise_chunk(3)
-        for e in range(E):
-            interleave_w2(e)
-        for e in range(E):
-            quantise_w2(e)
+        interleave_w2(0, nc.vector.tensor_copy)
+        quantise_w2(0)
         for hf in range(HALVES):
             b_bank[0, hf] = first_layer(0, W3, hf, "b_bank")
         interleave_chunk(4)
@@ -259,6 +257,8 @@ def tile_routed_moe_kernel(tc, xT, w1, w3, w2, gate, offs, out):
         y_sb_0 = late[:, HALVES * PACK * HALF:]
         for hf in range(HALVES):
             nc.scalar.copy(out=y_sb_0[:, hf * HALF:(hf + 1) * HALF], in_=y_bank[0, hf][:])
+        interleave_w2(1, nc.scalar.copy)
+        quantise_w2(1)
         for hf in range(HALVES):
             silu(1, hf, a_banks[hf], late[:, hf * PACK * HALF:(hf + 1) * PACK * HALF])
         y_sb_1 = keep.tile([P, C], F32, name="y_sb_1")

@@ -69,9 +69,11 @@ def tile_routed_moe_kernel(tc, xT, w1, w3, w2, gate, offs, out):
                 )
                 first += width
 
-        def load_w2(e):
-            w2_raw[e] = keep.tile([P, PACK, N], F32, name="w2_raw_%d" % e)
-            nc.sync.dma_start(out=w2_raw[e][:], in_=w2[e].rearrange("(p j) n -> p j n", j=PACK))
+        def load_w2():
+            tile = keep.tile([P, E, PACK, N], F32, name="w2_raw")
+            nc.sync.dma_start(out=tile[:], in_=w2.rearrange("e (p j) n -> p e j n", j=PACK))
+            for e in range(E):
+                w2_raw[e] = tile[:, e, :, :]
 
         offs_sb = keep.tile([P, SLOTS // 16], U16, name="offs_sb")
         nc.sync.dma_start(offs_sb[:], offs)
@@ -81,10 +83,9 @@ def tile_routed_moe_kernel(tc, xT, w1, w3, w2, gate, offs, out):
         load_tokens(1)
         load_chunk(2)
         load_chunk(3)
-        load_w2(0)
         for index in range(4, 8):
             load_chunk(index)
-        load_w2(1)
+        load_w2()
         gate_sb = keep.tile([P, SLOTS], F32, name="gate_sb")
         nc.sync.dma_start(out=gate_sb[:], in_=gate)
 
@@ -106,7 +107,6 @@ def tile_routed_moe_kernel(tc, xT, w1, w3, w2, gate, offs, out):
         wg = {}
         b_bank = {}
         hg = {}
-        y_bank = {}
 
         def tokens(g):
             g4 = work.tile([P, PACK, SLOTS], F32, name="g4")
@@ -127,11 +127,11 @@ def tile_routed_moe_kernel(tc, xT, w1, w3, w2, gate, offs, out):
                 in_=xg[:].rearrange("p c t -> p (c t)"),
             )
 
-        def interleave_w2(e, copy):
+        def interleave_w2(e):
             w2g[e] = work.tile([P, N, PACK], BF16, name="w2g", align_bytes=64)
-            copy(
+            nc.vector.tensor_copy(
                 out=w2g[e][:].rearrange("p (c i) j -> p c j i", i=4),
-                in_=w2_raw[e][:].rearrange("p j (c i) -> p c j i", i=4),
+                in_=w2_raw[e].rearrange("p j (c i) -> p c j i", i=4),
             )
 
         def quantise_w2(e):
@@ -193,17 +193,17 @@ def tile_routed_moe_kernel(tc, xT, w1, w3, w2, gate, offs, out):
                 op=MULT,
             )
 
-        def second_layer(e, hf):
-            h_codes = hp.tile([P, HALF], U32, name="h_codes", align_bytes=64)
-            h_scales = hp.tile([P, HALF], U8, name="h_scales", align_bytes=64)
+        def second_layer(e, h_grouped, slots, y_dst):
+            h_codes = hp.tile([P, slots], U32, name="h_codes_%d" % slots, align_bytes=64)
+            h_scales = hp.tile([P, slots], U8, name="h_scales_%d" % slots, align_bytes=64)
             nc.vector.quantize_mx(
                 out=h_codes[:].bitcast(FP8X4),
                 scales=h_scales[:],
-                in_=hg[e, hf].rearrange("p n s -> p (n s)"),
+                in_=h_grouped.rearrange("p n s -> p (n s)"),
             )
-            y_bank[e, hf] = psum.tile([P, HALF], F32, name="y_bank")
+            y_bank = psum.tile([P, slots], F32, name="y_bank")
             nc.tensor.matmul_mx(
-                out=y_bank[e, hf][:],
+                out=y_bank[:],
                 lhsT=w2_codes[e][:].bitcast(FP8X4),
                 lhsT_scale=w2_scales[e][:],
                 rhs=h_codes[:].bitcast(FP8X4),
@@ -211,6 +211,7 @@ def tile_routed_moe_kernel(tc, xT, w1, w3, w2, gate, offs, out):
                 start=True,
                 stop=True,
             )
+            nc.scalar.copy(out=y_dst, in_=y_bank[:])
 
         def scatter(e, y_sb):
             nc.vector.tensor_tensor(
@@ -233,8 +234,6 @@ def tile_routed_moe_kernel(tc, xT, w1, w3, w2, gate, offs, out):
             silu(0, hf, a_bank, sil_0[:])
         interleave_chunk(3)
         quantise_chunk(3)
-        interleave_w2(0, nc.vector.tensor_copy)
-        quantise_w2(0)
         for hf in range(HALVES):
             b_bank[0, hf] = first_layer(0, W3, hf, "b_bank")
         interleave_chunk(4)
@@ -242,8 +241,6 @@ def tile_routed_moe_kernel(tc, xT, w1, w3, w2, gate, offs, out):
         for hf in range(HALVES):
             hg[0, hf] = hg_0[:, hf, :, :]
             hidden(0, hf)
-        for hf in range(HALVES):
-            second_layer(0, hf)
         quantise_chunk(4)
         interleave_chunk(5)
         quantise_chunk(5)
@@ -254,24 +251,24 @@ def tile_routed_moe_kernel(tc, xT, w1, w3, w2, gate, offs, out):
             interleave_chunk(index)
             quantise_chunk(index)
         late = keep.tile([P, HALVES * PACK * HALF + C], F32, name="late", tag="w_raw_7_1", align_bytes=64)
-        y_sb_0 = late[:, HALVES * PACK * HALF:]
-        for hf in range(HALVES):
-            nc.scalar.copy(out=y_sb_0[:, hf * HALF:(hf + 1) * HALF], in_=y_bank[0, hf][:])
-        interleave_w2(1, nc.scalar.copy)
-        quantise_w2(1)
         for hf in range(HALVES):
             silu(1, hf, a_banks[hf], late[:, hf * PACK * HALF:(hf + 1) * PACK * HALF])
-        y_sb_1 = keep.tile([P, C], F32, name="y_sb_1")
         for hf in range(HALVES):
             b_bank[1, hf] = first_layer(1, W3, hf, "b_bank")
-        scatter(0, y_sb_0)
+        for e in range(E):
+            interleave_w2(e)
+        for e in range(E):
+            quantise_w2(e)
         for hf in range(HALVES):
             hg_1 = hp.tile([P, HALF, PACK], BF16, name="hg_1", align_bytes=64)
             hg[1, hf] = hg_1[:]
             hidden(1, hf)
+        y_sb_0 = late[:, HALVES * PACK * HALF:]
+        second_layer(0, hg_0[:].rearrange("p h n s -> p (h n) s"), C, y_sb_0)
+        y_sb_1 = keep.tile([P, C], F32, name="y_sb_1")
         for hf in range(HALVES):
-            second_layer(1, hf)
-            nc.scalar.copy(out=y_sb_1[:, hf * HALF:(hf + 1) * HALF], in_=y_bank[1, hf][:])
+            second_layer(1, hg[1, hf], HALF, y_sb_1[:, hf * HALF:(hf + 1) * HALF])
+        scatter(0, y_sb_0)
         scatter(1, y_sb_1[:])
 
         nc.sync.dma_start(out=out, in_=win[:])

@@ -127,15 +127,15 @@ def tile_routed_moe_kernel(tc, xT, w1, w3, w2, gate, offs, out):
                 in_=xg[:].rearrange("p c t -> p (c t)"),
             )
 
-        def interleave_w2(e):
+        def interleave_w2(e, copy):
             w2g[e] = work.tile([P, N, PACK], BF16, name="w2g", align_bytes=64)
-            nc.vector.tensor_copy(
+            copy(
                 out=w2g[e][:].rearrange("p (c i) j -> p c j i", i=4),
                 in_=w2_raw[e].rearrange("p j (c i) -> p c j i", i=4),
             )
 
-        def quantise_w2(e):
-            w2_codes[e] = keep.tile([P, N], U32, name="w2_codes_%d" % e, align_bytes=64)
+        def quantise_w2(e, tag):
+            w2_codes[e] = keep.tile([P, N], U32, name="w2_codes_%d" % e, tag=tag, align_bytes=64)
             w2_scales[e] = keep.tile([P, N], U8, name="w2_scales_%d" % e, align_bytes=64)
             nc.vector.quantize_mx(
                 out=w2_codes[e][:].bitcast(FP8X4),
@@ -155,15 +155,18 @@ def tile_routed_moe_kernel(tc, xT, w1, w3, w2, gate, offs, out):
                 )
                 first += m_rows
 
-        def quantise_chunk(index):
+        def quantise_chunk(index, parts=1):
             key = CHUNKS[index]
             w_codes[key] = keep.tile([P, H], U32, name="w_codes_%d" % index, align_bytes=64)
             w_scales[key] = keep.tile([P, H], U8, name="w_scales_%d" % index, align_bytes=64)
-            nc.vector.quantize_mx(
-                out=w_codes[key][:].bitcast(FP8X4),
-                scales=w_scales[key][:],
-                in_=wg[index][:].rearrange("p c j -> p (c j)"),
-            )
+            width = H // parts
+            for part in range(parts):
+                cols = slice(part * width, (part + 1) * width)
+                nc.vector.quantize_mx(
+                    out=w_codes[key][:, cols].bitcast(FP8X4),
+                    scales=w_scales[key][:, cols],
+                    in_=wg[index][:, cols, :].rearrange("p c j -> p (c j)"),
+                )
 
         def first_layer(e, mat, hf, name):
             bank = psum.tile([P, PACK, HALF], F32, name=name)
@@ -247,28 +250,31 @@ def tile_routed_moe_kernel(tc, xT, w1, w3, w2, gate, offs, out):
         a_banks = {}
         for hf in range(HALVES):
             a_banks[hf] = first_layer(1, W1, hf, "a_bank")
-        for index in (6, 7):
-            interleave_chunk(index)
-            quantise_chunk(index)
-        late = keep.tile([P, HALVES * PACK * HALF + C], F32, name="late", tag="w_raw_7_1", align_bytes=64)
-        for hf in range(HALVES):
-            silu(1, hf, a_banks[hf], late[:, hf * PACK * HALF:(hf + 1) * PACK * HALF])
+        interleave_chunk(6)
+        quantise_chunk(6)
+        interleave_chunk(7)
+        quantise_chunk(7, parts=2)
+        sil_1 = {}
+        for hf, tag in enumerate(("w_raw_7_1", "w_raw_7_0")):
+            sil_1[hf] = keep.tile([P, PACK * HALF], F32, name="sil_1_%d" % hf, tag=tag, align_bytes=64)
+            silu(1, hf, a_banks[hf], sil_1[hf][:])
         for hf in range(HALVES):
             b_bank[1, hf] = first_layer(1, W3, hf, "b_bank")
-        for e in range(E):
-            interleave_w2(e)
-        for e in range(E):
-            quantise_w2(e)
+        y_sb_0 = keep.tile([P, C], F32, name="y_sb_0")
+        y_sb_1 = keep.tile([P, C], F32, name="y_sb_1")
+        interleave_w2(0, nc.vector.tensor_copy)
+        quantise_w2(0, "w2_codes_0")
+        interleave_w2(1, nc.scalar.copy)
         for hf in range(HALVES):
             hg_1 = hp.tile([P, HALF, PACK], BF16, name="hg_1", align_bytes=64)
             hg[1, hf] = hg_1[:]
             hidden(1, hf)
-        y_sb_0 = late[:, HALVES * PACK * HALF:]
-        second_layer(0, hg_0[:].rearrange("p h n s -> p (h n) s"), C, y_sb_0)
-        y_sb_1 = keep.tile([P, C], F32, name="y_sb_1")
+            if hf == 0:
+                quantise_w2(1, "w_raw_7_1")
+        second_layer(0, hg_0[:].rearrange("p h n s -> p (h n) s"), C, y_sb_0[:])
         for hf in range(HALVES):
             second_layer(1, hg[1, hf], HALF, y_sb_1[:, hf * HALF:(hf + 1) * HALF])
-        scatter(0, y_sb_0)
+        scatter(0, y_sb_0[:])
         scatter(1, y_sb_1[:])
 
         nc.sync.dma_start(out=out, in_=win[:])

@@ -24,10 +24,10 @@ HALVES = C // HALF
 
 W1, W3 = 0, 1
 CHUNKS = (
-    (0, W1, 0), (0, W3, 0), (0, W1, 1), (0, W3, 1),
+    (0, W1, 0), (0, W1, 1), (0, W3, 0), (0, W3, 1),
     (1, W1, 0), (1, W1, 1), (1, W3, 0), (1, W3, 1),
 )
-CHUNK_VECTOR_SHARE = ((64,), (64,), (64,), (64,), (112,), (32,), (64,), (56, 16))
+CHUNK_VECTOR_SHARE = ((64,), (64,), (64,), (64,), (112,), (48,), (80,), (56, 16))
 CHUNK_PIECE_ROWS = ((128,), (128,), (128,), (128,), (128,), (128,), (128,), (96, 32))
 TOKEN_VECTOR_SHARE = (64, 96)
 
@@ -78,11 +78,11 @@ def tile_routed_moe_kernel(tc, xT, w1, w3, w2, gate, offs, out):
         offs_sb = keep.tile([P, SLOTS // 16], U16, name="offs_sb")
         nc.sync.dma_start(offs_sb[:], offs)
         load_tokens(0)
-        load_chunk(0)
-        load_chunk(1)
+        for index in range(2):
+            load_chunk(index)
         load_tokens(1)
-        load_chunk(2)
-        load_chunk(3)
+        for index in range(2, 4):
+            load_chunk(index)
         for index in range(4, 8):
             load_chunk(index)
         load_w2()
@@ -144,7 +144,10 @@ def tile_routed_moe_kernel(tc, xT, w1, w3, w2, gate, offs, out):
             )
 
         def interleave_chunk(index):
-            wg[index] = wgp.tile([P, H, PACK], BF16, name="wg", align_bytes=64)
+            if index == len(CHUNKS) - 1:
+                wg[index] = keep.tile([P, H, PACK], BF16, name="wg_last", align_bytes=64)
+            else:
+                wg[index] = wgp.tile([P, H, PACK], BF16, name="wg", align_bytes=64)
             first = 0
             for part, m_rows in enumerate(CHUNK_PIECE_ROWS[index]):
                 shared_copy(
@@ -197,7 +200,10 @@ def tile_routed_moe_kernel(tc, xT, w1, w3, w2, gate, offs, out):
             )
 
         def second_layer(e, h_grouped, slots, y_dst):
-            h_codes = hp.tile([P, slots], U32, name="h_codes_%d" % slots, align_bytes=64)
+            if e == 0:
+                h_codes = keep.tile([P, slots], U32, name="h_codes_0", tag="wg_last", align_bytes=64)
+            else:
+                h_codes = hp.tile([P, slots], U32, name="h_codes_1", align_bytes=64)
             h_scales = hp.tile([P, slots], U8, name="h_scales_%d" % slots, align_bytes=64)
             nc.vector.quantize_mx(
                 out=h_codes[:].bitcast(FP8X4),
@@ -225,18 +231,20 @@ def tile_routed_moe_kernel(tc, xT, w1, w3, w2, gate, offs, out):
             )
 
         tokens(0)
-        for index in (0, 1):
+        for index in range(2):
             interleave_chunk(index)
             quantise_chunk(index)
         tokens(1)
         interleave_chunk(2)
         quantise_chunk(2)
+        a_banks = {}
         for hf in range(HALVES):
-            a_bank = first_layer(0, W1, hf, "a_bank")
-            sil_0 = hp.tile([P, PACK * HALF], F32, name="sil_0")
-            silu(0, hf, a_bank, sil_0[:])
+            a_banks[hf] = first_layer(0, W1, hf, "a_bank")
         interleave_chunk(3)
         quantise_chunk(3)
+        sil_0 = keep.tile([P, HALVES, PACK * HALF], F32, name="sil_0", tag="w_raw_3_0", align_bytes=64)
+        for hf in range(HALVES):
+            silu(0, hf, a_banks[hf], sil_0[:, hf, :])
         for hf in range(HALVES):
             b_bank[0, hf] = first_layer(0, W3, hf, "b_bank")
         interleave_chunk(4)
@@ -247,7 +255,6 @@ def tile_routed_moe_kernel(tc, xT, w1, w3, w2, gate, offs, out):
         quantise_chunk(4)
         interleave_chunk(5)
         quantise_chunk(5)
-        a_banks = {}
         for hf in range(HALVES):
             a_banks[hf] = first_layer(1, W1, hf, "a_bank")
         interleave_chunk(6)

from contextlib import ExitStack

import concourse.mybir as mybir

K, T, E, C, H, N = 1024, 2048, 2, 256, 512, 128
FLOPS = 2 * E * C * (2 * K * H + H * N)

F32 = mybir.dt.float32
BF16 = mybir.dt.bfloat16
U32 = mybir.dt.uint32
U16 = mybir.dt.uint16
U8 = mybir.dt.uint8
FP8X4 = mybir.dt.float8_e4m3fn_x4
MULT = mybir.AluOpType.mult
SILU = mybir.ActivationFunctionType.Silu

P = 128
PACK = 4
K_PASS = P * PACK
PASSES = K // K_PASS
SLOTS = E * C
HALF = 128
HALVES = C // HALF

W1, W3 = 0, 1
CHUNKS = (
    (0, W1, 0), (0, W1, 1), (0, W3, 0), (0, W3, 1),
    (1, W1, 0), (1, W1, 1), (1, W3, 0), (1, W3, 1),
)
CHUNK_VECTOR_SHARE = ((64,), (64,), (64,), (64,), (112,), (48,), (80,), (56, 16))
CHUNK_PIECE_ROWS = ((128,), (128,), (128,), (128,), (128,), (128,), (128,), (96, 32))
TOKEN_VECTOR_SHARE = (64, 96)


def shared_copy(nc, dst, src, vector_share):
    nc.vector.tensor_copy(out=dst[:, 0:vector_share, :, :], in_=src[:, 0:vector_share, :, :])
    nc.scalar.copy(out=dst[:, vector_share:, :, :], in_=src[:, vector_share:, :, :])


def tile_routed_moe_kernel(tc, xT, w1, w3, w2, gate, offs, out):
    nc = tc.nc
    with ExitStack() as ctx:
        keep = ctx.enter_context(tc.tile_pool(name="keep", bufs=1))
        work = ctx.enter_context(tc.tile_pool(name="work", bufs=2))
        wgp = ctx.enter_context(tc.tile_pool(name="wgp", bufs=3))
        hp = ctx.enter_context(tc.tile_pool(name="hp", bufs=4))
        psum = ctx.enter_context(tc.psum_pool(name="psum", bufs=2))

        x_plane = {}
        w_raw = {}
        w2_raw = {}
        planes = xT.rearrange("(g p t) n -> g p t n", p=P, t=PACK)

        def load_tokens(g):
            for t in range(PACK):
                x_plane[g, t] = keep.tile([P, T], F32, name="x_plane_%d_%d" % (g, t))
                nc.sync.dma_start(out=x_plane[g, t][:], in_=planes[g, :, t, :])

        def load_chunk(index):
            e, mat, g = CHUNKS[index]
            rows = (w1, w3)[mat][e, g * K_PASS:(g + 1) * K_PASS, :]
            first = 0
            for part, m_rows in enumerate(CHUNK_PIECE_ROWS[index]):
                width = PACK * m_rows
                w_raw[index, part] = keep.tile([P, PACK, width], F32, name="w_raw_%d_%d" % (index, part), align_bytes=64)
                nc.sync.dma_start(
                    out=w_raw[index, part][:],
                    in_=rows[:, first:first + width].rearrange("(p j) c -> p j c", j=PACK),
                )
                first += width

        def load_w2():
            tile = keep.tile([P, E, PACK, N], F32, name="w2_raw")
            nc.sync.dma_start(out=tile[:], in_=w2.rearrange("e (p j) n -> p e j n", j=PACK))
            for e in range(E):
                w2_raw[e] = tile[:, e, :, :]

        offs_sb = keep.tile([P, SLOTS // 16], U16, name="offs_sb")
        nc.sync.dma_start(offs_sb[:], offs)
        load_tokens(0)
        for index in range(2):
            load_chunk(index)
        load_tokens(1)
        for index in range(2, 4):
            load_chunk(index)
        for index in range(4, 8):
            load_chunk(index)
        load_w2()
        gate_sb = keep.tile([P, SLOTS], F32, name="gate_sb")
        nc.sync.dma_start(out=gate_sb[:], in_=gate)

        warm_in = keep.tile([P, 1], F32, name="warm_in")
        warm_out = keep.tile([P, 1], F32, name="warm_out")
        nc.vector.memset(warm_in[:], 0.0)
        nc.scalar.activation(out=warm_out[:], in_=warm_in[:], func=SILU)
        win = keep.tile([P, T], F32, name="win")
        nc.vector.memset(win[:], 0.0)

        x_codes = {}
        x_scales = {}
        w2_codes = {}
        w2_scales = {}
        w_codes = {}
        w_scales = {}
        sil = {}
        w2g = {}
        wg = {}
        b_bank = {}
        hg = {}

        def tokens(g):
            g4 = work.tile([P, PACK, SLOTS], F32, name="g4")
            for t in range(PACK):
                nc.vector.tensor_copy(g4[:, t, :], x_plane[g, t][:].indirect(offs_sb[:]))
            xg = work.tile([P, SLOTS, PACK], BF16, name="xg", align_bytes=64)
            shared_copy(
                nc,
                xg[:].rearrange("p (c i) t -> p c t i", i=4),
                g4[:].rearrange("p t (c i) -> p c t i", i=4),
                TOKEN_VECTOR_SHARE[g],
            )
            x_codes[g] = keep.tile([P, SLOTS], U32, name="x_codes_%d" % g, align_bytes=64)
            x_scales[g] = keep.tile([P, SLOTS], U8, name="x_scales_%d" % g, align_bytes=64)
            nc.vector.quantize_mx(
                out=x_codes[g][:].bitcast(FP8X4),
                scales=x_scales[g][:],
                in_=xg[:].rearrange("p c t -> p (c t)"),
            )

        def interleave_w2(e, copy):
            w2g[e] = work.tile([P, N, PACK], BF16, name="w2g", align_bytes=64)
            copy(
                out=w2g[e][:].rearrange("p (c i) j -> p c j i", i=4),
                in_=w2_raw[e].rearrange("p j (c i) -> p c j i", i=4),
            )

        def quantise_w2(e, tag):
            w2_codes[e] = keep.tile([P, N], U32, name="w2_codes_%d" % e, tag=tag, align_bytes=64)
            w2_scales[e] = keep.tile([P, N], U8, name="w2_scales_%d" % e, align_bytes=64)
            nc.vector.quantize_mx(
                out=w2_codes[e][:].bitcast(FP8X4),
                scales=w2_scales[e][:],
                in_=w2g[e][:].rearrange("p c j -> p (c j)"),
            )

        def interleave_chunk(index):
            if index == len(CHUNKS) - 1:
                wg[index] = keep.tile([P, H, PACK], BF16, name="wg_last", align_bytes=64)
            else:
                wg[index] = wgp.tile([P, H, PACK], BF16, name="wg", align_bytes=64)
            first = 0
            for part, m_rows in enumerate(CHUNK_PIECE_ROWS[index]):
                shared_copy(
                    nc,
                    wg[index][:].rearrange("p (s m) j -> p m j s", s=PACK)[:, first:first + m_rows, :, :],
                    w_raw[index, part][:].rearrange("p j (m s) -> p m j s", s=PACK),
                    CHUNK_VECTOR_SHARE[index][part],
                )
                first += m_rows

        def quantise_chunk(index, parts=1):
            key = CHUNKS[index]
            w_codes[key] = keep.tile([P, H], U32, name="w_codes_%d" % index, align_bytes=64)
            w_scales[key] = keep.tile([P, H], U8, name="w_scales_%d" % index, align_bytes=64)
            width = H // parts
            for part in range(parts):
                cols = slice(part * width, (part + 1) * width)
                nc.vector.quantize_mx(
                    out=w_codes[key][:, cols].bitcast(FP8X4),
                    scales=w_scales[key][:, cols],
                    in_=wg[index][:, cols, :].rearrange("p c j -> p (c j)"),
                )

        def first_layer(e, mat, hf, name):
            bank = psum.tile([P, PACK, HALF], F32, name=name)
            cols = slice(e * C + hf * HALF, e * C + (hf + 1) * HALF)
            for s in range(PACK):
                for g in range(PASSES):
                    nc.tensor.matmul_mx(
                        out=bank[:, s, :],
                        lhsT=w_codes[e, mat, g][:, s * P:(s + 1) * P].bitcast(FP8X4),
                        lhsT_scale=w_scales[e, mat, g][:, s * P:(s + 1) * P],
                        rhs=x_codes[g][:, cols].bitcast(FP8X4),
                        rhs_scale=x_scales[g][:, cols],
                        start=(g == 0),
                        stop=(g == PASSES - 1),
                    )
            return bank

        def silu(e, hf, a_bank, dst):
            sil[e, hf] = dst.rearrange("p (n s) -> p n s", s=PACK)
            nc.scalar.activation(out=sil[e, hf], in_=a_bank[:].rearrange("p s n -> p n s"), func=SILU)

        def hidden(e, hf):
            nc.vector.tensor_tensor(
                out=hg[e, hf],
                in0=sil[e, hf],
                in1=b_bank[e, hf][:].rearrange("p s n -> p n s"),
                op=MULT,
            )

        def second_layer(e, h_grouped, slots, y_dst):
            if e == 0:
                h_codes = keep.tile([P, slots], U32, name="h_codes_0", tag="wg_last", align_bytes=64)
            else:
                h_codes = hp.tile([P, slots], U32, name="h_codes_1", align_bytes=64)
            h_scales = hp.tile([P, slots], U8, name="h_scales_%d" % slots, align_bytes=64)
            nc.vector.quantize_mx(
                out=h_codes[:].bitcast(FP8X4),
                scales=h_scales[:],
                in_=h_grouped.rearrange("p n s -> p (n s)"),
            )
            y_bank = psum.tile([P, slots], F32, name="y_bank")
            nc.tensor.matmul_mx(
                out=y_bank[:],
                lhsT=w2_codes[e][:].bitcast(FP8X4),
                lhsT_scale=w2_scales[e][:],
                rhs=h_codes[:].bitcast(FP8X4),
                rhs_scale=h_scales[:],
                start=True,
                stop=True,
            )
            nc.scalar.copy(out=y_dst, in_=y_bank[:])

        def scatter(e, y_sb):
            nc.vector.tensor_tensor(
                win[:].indirect(offs_sb[:, e * (C // 16):(e + 1) * (C // 16)]),
                y_sb,
                gate_sb[:, e * C:(e + 1) * C],
                MULT,
            )

        tokens(0)
        for index in range(2):
            interleave_chunk(index)
            quantise_chunk(index)
        tokens(1)
        interleave_chunk(2)
        quantise_chunk(2)
        a_banks = {}
        for hf in range(HALVES):
            a_banks[hf] = first_layer(0, W1, hf, "a_bank")
        interleave_chunk(3)
        quantise_chunk(3)
        sil_0 = keep.tile([P, HALVES, PACK * HALF], F32, name="sil_0", tag="w_raw_3_0", align_bytes=64)
        for hf in range(HALVES):
            silu(0, hf, a_banks[hf], sil_0[:, hf, :])
        for hf in range(HALVES):
            b_bank[0, hf] = first_layer(0, W3, hf, "b_bank")
        interleave_chunk(4)
        hg_0 = keep.tile([P, HALVES, HALF, PACK], BF16, name="hg_0", tag="w_raw_4_0", align_bytes=64)
        for hf in range(HALVES):
            hg[0, hf] = hg_0[:, hf, :, :]
            hidden(0, hf)
        quantise_chunk(4)
        interleave_chunk(5)
        quantise_chunk(5)
        for hf in range(HALVES):
            a_banks[hf] = first_layer(1, W1, hf, "a_bank")
        interleave_chunk(6)
        quantise_chunk(6)
        interleave_chunk(7)
        quantise_chunk(7, parts=2)
        sil_1 = {}
        for hf, tag in enumerate(("w_raw_7_1", "w_raw_7_0")):
            sil_1[hf] = keep.tile([P, PACK * HALF], F32, name="sil_1_%d" % hf, tag=tag, align_bytes=64)
            silu(1, hf, a_banks[hf], sil_1[hf][:])
        for hf in range(HALVES):
            b_bank[1, hf] = first_layer(1, W3, hf, "b_bank")
        y_sb_0 = keep.tile([P, C], F32, name="y_sb_0")
        y_sb_1 = keep.tile([P, C], F32, name="y_sb_1")
        interleave_w2(0, nc.vector.tensor_copy)
        quantise_w2(0, "w2_codes_0")
        interleave_w2(1, nc.scalar.copy)
        for hf in range(HALVES):
            hg_1 = hp.tile([P, HALF, PACK], BF16, name="hg_1", align_bytes=64)
            hg[1, hf] = hg_1[:]
            hidden(1, hf)
            if hf == 0:
                quantise_w2(1, "w_raw_7_1")
        second_layer(0, hg_0[:].rearrange("p h n s -> p (h n) s"), C, y_sb_0[:])
        for hf in range(HALVES):
            second_layer(1, hg[1, hf], HALF, y_sb_1[:, hf * HALF:(hf + 1) * HALF])
        scatter(0, y_sb_0[:])
        scatter(1, y_sb_1[:])

        nc.sync.dma_start(out=out, in_=win[:])
